import numpy as np
CORES = [120,121,122,123,124,125,126,127,128,129,130,131]
N = 12
PERM = [[0,11],[1,10],[2,9],[3,8],[4,7],[5,6],[6,5],[7,4],[8,3],[9,2],[10,1],[11,0]]
def setup_inputs(rng):
    return {"x": rng.standard_normal((N, 128, 4), dtype=np.float32)}
def reference(x):
    y = np.empty_like(x)
    for s, d in PERM:
        y[d] = x[s]
    return {"y": y}

SCRATCH = {
    "stage": ("dram", [128, 4], "float32"),
    "hop": ("dram", [128, 4], "float32"),
    "land": ("dram", [128, 4], "float32"),
}
SEMAPHORES = ["loaded", "sent", "hopped", "arrived", "stored"]

ENGINES = 4
MASK = (1 << ENGINES) - 1
PORT_CORES = (2, 6, 3, 7)


def routes(T, topo):
    group = set(T.cores)
    used = set()
    out = []
    for s, d in T.tables["PERM"]:
        a, b = T.cores[s], T.cores[d]
        if a == b or topo.may_write(a, b):
            out.append((a, None, b))
            continue
        base = topo.host(b) * 128 + (topo.chip(b) ^ 1) * 8
        free = [base + k for k in PORT_CORES if base + k not in used and base + k != a]
        idle = [c for c in free if c not in group]
        r = (idle or free)[0]
        used.add(r)
        out.append((a, r, b))
    return out


def rank_program(g, core, T, topo):
    plan = routes(T, topo)
    sem = T.sem
    sent = 0

    def write(dst, out_ap, in_ap, remote_sem):
        rid, pid = topo.addr(dst, core)
        g.remote_dma(out_ap, in_ap, remote_sem, sem.sent, pid, rid, MASK)

    for a, r, b in plan:
        if a == core and b == core:
            g.sync.dma_start(T.y[:], T.x[:]).then_inc(sem.stored, 16)
            g.sync.wait_ge(sem.stored, 16)
            return

    for a, r, b in plan:
        if a == core:
            g.sync.dma_start(T.stage[:], T.x[:]).then_inc(sem.loaded, 16)
            g.wait_ge(sem.loaded, 16)
            if r is None:
                write(b, T.land[:], T.stage[:], sem.arrived)
            else:
                write(r, T.hop[:], T.stage[:], sem.hopped)
            sent += ENGINES

    for a, r, b in plan:
        if r == core:
            g.wait_ge(sem.hopped, ENGINES)
            write(b, T.land[:], T.hop[:], sem.arrived)
            sent += ENGINES

    for a, r, b in plan:
        if b == core:
            g.scalar.wait_ge(sem.arrived, ENGINES)
            g.scalar.dma_start(T.y[:], T.land[:]).then_inc(sem.stored, 16)
            g.scalar.wait_ge(sem.stored, 16)

    if sent:
        g.wait_ge(sem.sent, sent)
